import numpy as np
import ml_dtypes


def mxq(x, axis, fmt="e4m3"):
    dtype, down = {"e4m3": (ml_dtypes.float8_e4m3fn, 7), "e5m2": (ml_dtypes.float8_e5m2, 14)}[fmt]
    v = np.moveaxis(np.asarray(x, np.float32).astype(ml_dtypes.bfloat16).astype(np.float64), axis, -1)
    blocks = v.reshape(v.shape[:-1] + (-1, 32))
    amax = np.abs(blocks).max(-1, keepdims=True)
    byte = np.maximum(np.where(amax > 0, np.frexp(amax)[1] - 1 + 127, 0) - down, 1)
    scale = np.exp2(byte - 127.0)
    codes = (blocks / scale).astype(np.float32).astype(dtype).astype(np.float64)
    return np.moveaxis((codes * scale).reshape(v.shape), -1, axis)


WIDE = False


def mx_kscale(k):
    if not WIDE:
        return np.ones(k)
    levels = np.array([10, -10, 5, -5, 0])
    if k % 512:
        return np.exp2(np.random.permutation(np.resize(levels, k // 32))).repeat(32)
    a = np.empty((k // 512, 16))
    for p in range(k // 512):
        a[p, :8] = np.random.permutation(np.resize(levels, 8))
        for g in range(8):
            far = levels[np.abs(levels - a[p, g]) >= 10]
            a[p, g + 8] = far[np.random.randint(len(far))]
    return np.exp2(a.ravel()).repeat(32)


def f64(x):
    return np.asarray(x).astype(np.float64)


def striped(idx):
    return np.tile(idx.reshape(-1, 16).T, (8, 1)).astype(np.uint16)


def unstriped(offs):
    return offs[:16].T.reshape(-1).astype(np.int64)


E2M1 = np.array([0.0, 0.5, 1.0, 1.5, 2.0, 3.0, 4.0, 6.0, -0.0, -0.5, -1.0, -1.5, -2.0, -3.0, -4.0, -6.0])


def pack_weight(w, fmt):
    k, n = w.shape
    w = f64(np.asarray(w, np.float32).astype(ml_dtypes.bfloat16)).reshape(k // 32, 32, n)
    amax = np.abs(w).max(1)
    if fmt == "e4m3":
        byte = np.frexp(amax)[1] - 1 + 127 - 7
    else:
        mant, ex = np.frexp(amax / 6.0)
        byte = np.where(mant > 0.5, ex, ex - 1) + 127
    byte = np.clip(np.where(amax > 0, byte, 1), 1, 254)
    scaled = (w * np.exp2(127.0 - byte)[:, None, :]).reshape(k, n).astype(np.float32)
    by_word = np.ascontiguousarray(scaled.reshape(k // 512, 128, 4, n).transpose(0, 1, 3, 2))
    if fmt == "e4m3":
        words = by_word.astype(ml_dtypes.float8_e4m3fn).view(np.uint8)
    else:
        c = by_word.astype(ml_dtypes.float4_e2m1fn).view(np.uint8) & 0xF
        words = (c[..., 0::2] | (c[..., 1::2] << 4)).reshape(k // 512, 128, 2 * n)
    return np.ascontiguousarray(words), np.ascontiguousarray(byte.astype(np.uint8).reshape(k // 512, 16, n))


def unpack_weight(words, scales, fmt):
    g, _, n = scales.shape
    words = np.ascontiguousarray(words).reshape(g, 128, n, -1)
    if fmt == "e4m3":
        vals = words.view(ml_dtypes.float8_e4m3fn).astype(np.float64)
    else:
        nib = np.empty((g, 128, n, 4), np.uint8)
        nib[..., 0::2] = words & 0xF
        nib[..., 1::2] = words >> 4
        vals = E2M1[nib]
    vals = vals * np.repeat(np.exp2(scales.astype(np.float64) - 127.0), 8, axis=1)[..., None]
    return vals.transpose(0, 1, 3, 2).reshape(g * 512, n)


def gelu(v):
    return 0.5 * v * (1.0 + np.tanh(np.sqrt(2.0 / np.pi) * (v + 0.044715 * v**3)))


def often(T, S):
    return np.random.permutation(T)[(T * np.random.uniform(0, 1, S) ** 4).astype(np.int64)]


T, S, P, K1, K2, K3, H, N = 2048, 1024, 512, 1024, 512, 512, 1024, 256

def setup_inputs():
    n = np.random.standard_normal
    s1, s2, s3 = mx_kscale(K1)[:, None], mx_kscale(K2)[:, None], mx_kscale(K3)[:, None]
    u = mx_kscale(H)[:, None]
    d = {}
    d["tab_words"], d["tab_scales"] = pack_weight(n((K1, T)) * s1, "e4m3")
    d["tab2_words"], d["tab2_scales"] = pack_weight(n((K2, T)) * s2, "e4m3")
    d["tab3_words"], d["tab3_scales"] = pack_weight(n((K3, T)) * s3, "e4m3")
    d["offs"] = striped(np.random.permutation(T)[:S])
    d["offs2"] = striped(np.random.permutation(T)[:S])
    d["offs3"] = striped(np.random.permutation(T)[:S])
    d["pos1"] = striped(np.random.permutation(S)[:P])
    d["pos2"] = striped(often(S, P))
    d["pos3"] = striped(often(S, P))
    d["w1"] = (n((K1, H)) / K1 ** 0.5 / s1 * u.T).astype(np.float32)
    d["w2_words"], d["w2_scales"] = pack_weight(n((K2, H)) / K2 ** 0.5 / s2, "e2m1")
    d["w3_words"], d["w3_scales"] = pack_weight(1.5 * n((K3, H)) / K3 ** 0.5 / s3, "e4m3")
    d["rel"] = (n((H, P)) * u).astype(np.float32)
    d["gain"] = (1.3 * np.exp(0.3 * n(H)) * u[:, 0]).astype(np.float32)
    d["w4"] = (n((H, N)) / H ** 0.5 / u).astype(np.float32)
    return d

def reference(tab_words, tab_scales, tab2_words, tab2_scales, tab3_words, tab3_scales, offs, offs2, offs3,
              pos1, pos2, pos3, w1, w2_words, w2_scales, w3_words, w3_scales, rel, gain, w4):
    v = unpack_weight(tab_words, tab_scales, "e4m3")[:, unstriped(offs)]
    v2 = unpack_weight(tab2_words, tab2_scales, "e4m3")[:, unstriped(offs2)]
    v3 = unpack_weight(tab3_words, tab3_scales, "e4m3")[:, unstriped(offs3)]
    a = mxq(f64(w1), 0, "e4m3").T @ v
    b = unpack_weight(w2_words, w2_scales, "e2m1").T @ v2
    d = unpack_weight(w3_words, w3_scales, "e4m3").T @ v3
    seen = a[:, unstriped(pos1)] + f64(rel) * b[:, unstriped(pos2)]
    usual = f64(gain)[:, None] * np.tanh(d[:, unstriped(pos3)])
    z = seen - usual
    y = mxq(f64(w4), 0, "e4m3").T @ mxq(z, 0, "e4m3")
    return np.abs(y)

@@ -1,0 +1,279 @@
+from contextlib import ExitStack
+
+import concourse.mybir as mybir
+from concourse.masks import make_identity
+
+T, S, J, K1, K2, K3, H, N = 2048, 1024, 512, 1024, 512, 512, 1024, 256
+FLOPS = 2 * H * S * (K1 + K2 + K3) + 2 * H * N * J
+
+F32 = mybir.dt.float32
+BF16 = mybir.dt.bfloat16
+I32 = mybir.dt.int32
+U32 = mybir.dt.uint32
+U16 = mybir.dt.uint16
+U8 = mybir.dt.uint8
+FP8X4 = mybir.dt.float8_e4m3fn_x4
+FP4X4 = mybir.dt.float4_e2m1fn_x4
+ACT = mybir.ActivationFunctionType
+ALU = mybir.AluOpType
+
+P = 128
+BANK = 512
+TILES = H // P
+HALF = J // 2
+
+
+def tile_list_deposit_suspicion_scores_kernel(
+    tc, tab_words, tab_scales, tab2_words, tab2_scales, tab3_words, tab3_scales, offs, offs2, offs3,
+    pos1, pos2, pos3, w1, w2_words, w2_scales, w3_words, w3_scales, rel, gain, w4, out,
+):
+    nc = tc.nc
+    with ExitStack() as ctx:
+        keep = ctx.enter_context(tc.tile_pool(name="keep", bufs=1))
+        ring = ctx.enter_context(tc.tile_pool(name="ring", bufs=4))
+        psum = ctx.enter_context(tc.psum_pool(name="psum", bufs=8))
+
+        def held(shape, dtype, name):
+            return keep.tile(shape, dtype, name=name, align_bytes=64)
+
+        def load_list(src, name):
+            t = keep.tile([P, src.shape[1]], U16, name=name)
+            nc.sync.dma_start(t[:], src)
+            return t
+
+        def load_words(src, name):
+            t = held([P, src.shape[1]], U32, name)
+            nc.sync.dma_start(t[:].bitcast(I32), src.rearrange("p n i -> p (n i)").bitcast(I32))
+            return t
+
+        def load_scales(queue, zeroer, src, name):
+            passes, width = src.shape[0], src.shape[2]
+            t = held([P, width], U8, name)
+            zeroer.memset(t[:].bitcast(I32), 0)
+            rows = src.bitcast(I32)
+            for q in range(4):
+                queue.dma_start(t[32 * q : 32 * q + 4 * passes, :].bitcast(I32), rows[:, 4 * q : 4 * q + 4, :])
+            return t
+
+        def gather(window, lst, dtype, name):
+            t = held([P, S], dtype, name)
+            nc.vector.tensor_copy(t[:], window[:].indirect(lst[:]))
+            return t
+
+        def deal(src, name):
+            words = src[:].bitcast(I32)
+            t = held([P, words.shape[1]], I32, name)
+            nc.vector.tensor_copy(
+                t[:].rearrange("p (b t q i) -> p b t q i", b=2, t=4, q=16),
+                words.rearrange("p (b q t i) -> p b t q i", b=2, t=4, q=16),
+            )
+            return t
+
+        offs3_t = load_list(offs3, "offs3_t")
+        tab3_s = held([P, T], U8, "tab3_s")
+        rows3 = tab3_scales.bitcast(I32)
+        for q in range(4):
+            nc.scalar.dma_start(
+                tab3_s[32 * q : 32 * q + 32, :].bitcast(I32),
+                rows3[:, 4 * q : 4 * q + 4, :].to_broadcast([8, 4, T // 4]),
+            )
+        tab3_w = load_words(tab3_words[0], "tab3_w")
+        w3_w = load_words(w3_words[0], "w3_w")
+        offs2_t = load_list(offs2, "offs2_t")
+        w3_s = load_scales(nc.scalar, nc.vector, w3_scales, "w3_s")
+        tab2_s = load_scales(nc.scalar, nc.vector, tab2_scales, "tab2_s")
+        w2_s = load_scales(nc.scalar, nc.vector, w2_scales, "w2_s")
+
+        w1_raw = {}
+
+        def load_w1(a, b):
+            t = ring.tile([P, 4, BANK], F32, name="raw")
+            nc.sync.dma_start(
+                t[:], w1[512 * a : 512 * (a + 1), BANK * b : BANK * (b + 1)].rearrange("(p e) c -> p e c", e=4)
+            )
+            w1_raw[a, b] = t
+
+        tab2_w = load_words(tab2_words[0], "tab2_w")
+        load_w1(0, 0)
+        w2_w = held([P, 2 * H], U8, "w2_w")
+        nc.sync.dma_start(w2_w[:].bitcast(I32), w2_words[0].bitcast(I32))
+        pos3_t = load_list(pos3, "pos3_t")
+        pos2_t = load_list(pos2, "pos2_t")
+
+        gain_rows = held([P, P], F32, "gain_rows")
+        nc.gpsimd.memset(gain_rows[:], 0.0)
+        gain_v = gain.rearrange("(b q t i) -> b t q i", b=2, q=16, t=4)
+        for b in range(2):
+            nc.gpsimd.dma_start(gain_rows[4 * b : 4 * b + 4, :].rearrange("t (q i) -> t q i", q=16), gain_v[b])
+        ident = held([P, P], F32, "ident")
+        make_identity(nc, ident[:])
+
+        rel_v = rel.rearrange("(b q t i) j -> b t q i j", b=2, q=16, t=4)
+        rel_t = []
+
+        def load_rel(c):
+            t = held([P, J], F32, "rel%d" % c)
+            nc.sync.dma_start(t[:], rel_v[c // 4, c % 4])
+            rel_t.append(t)
+
+        load_rel(0)
+        load_rel(1)
+        load_w1(1, 0)
+        load_rel(2)
+        load_rel(3)
+        offs_t = load_list(offs, "offs_t")
+        pos1_t = load_list(pos1, "pos1_t")
+        load_w1(0, 1)
+        load_rel(4)
+        load_rel(5)
+        load_w1(1, 1)
+        load_rel(6)
+        load_rel(7)
+        tab_s = load_scales(nc.sync, nc.gpsimd, tab_scales, "tab_s")
+        tab_w = [load_words(tab_words[a], "tab_w%d" % a) for a in range(2)]
+        w4_raw = ring.tile([P, 2, 4, N], F32, name="raw")
+        w4_v = w4.rearrange("(b q t i) n -> b t q i n", b=2, q=16, t=4)
+        for c in range(TILES):
+            nc.sync.dma_start(w4_raw[:, c // 4, c % 4, :], w4_v[c // 4, c % 4])
+
+        warm = held([P, 8], F32, "warm")
+        nc.scalar.activation(warm[:, 0:1], ident[:, 0:1], ACT.Tanh)
+
+        gain_ps = psum.tile([P, BANK], F32, name="bank")
+        nc.tensor.transpose(gain_ps[:, 0:P], gain_rows[:], ident[:])
+        gain_t = held([P, TILES], F32, "gain_t")
+        nc.scalar.copy(gain_t[:], gain_ps[:, 0:TILES])
+
+        v3_s = gather(tab3_s, offs3_t, U8, "v3_s")
+        v3_w = gather(tab3_w, offs3_t, U32, "v3_w")
+        w3_wd = deal(w3_w, "w3_wd")
+        w3_sd = deal(w3_s, "w3_sd")
+        v2_s = gather(tab2_s, offs2_t, U8, "v2_s")
+        v2_w = gather(tab2_w, offs2_t, U32, "v2_w")
+        w2_wd = deal(w2_w, "w2_wd")
+        w2_sd = deal(w2_s, "w2_sd")
+
+        def product(c, passes, name):
+            win = ring.tile([P, S], F32, name=name)
+            for h in range(S // BANK):
+                cols = slice(BANK * h, BANK * (h + 1))
+                acc = psum.tile([P, BANK], F32, name="bank")
+                for n, (lw, ls, rw, rs) in enumerate(passes):
+                    nc.tensor.matmul_mx(
+                        out=acc[:], lhsT=lw, lhsT_scale=ls, rhs=rw[:, cols].bitcast(FP8X4), rhs_scale=rs[:, cols],
+                        start=(n == 0), stop=(n == len(passes) - 1),
+                    )
+                nc.scalar.copy(win[:, cols], acc[:])
+            return win
+
+        w1_bf = {}
+
+        def cast_w1(a, b):
+            t = ring.tile([P, 4 * BANK], BF16, name="bf", bufs=3, align_bytes=64)
+            nc.scalar.copy(
+                t[:].rearrange("p (t q i e) -> p t q e i", t=4, q=16, e=4),
+                w1_raw[a, b][:].rearrange("p e (q t i) -> p t q e i", t=4, q=16),
+            )
+            w1_bf[a, b] = t
+
+        def quantize(src, name):
+            width = src.shape[1] // 4
+            codes = held([P, width], U32, name + "_w")
+            scales = held([P, width], U8, name + "_s")
+            nc.vector.quantize_mx(out=codes[:].bitcast(FP8X4), scales=scales[:], in_=src)
+            return codes, scales
+
+        d_win, b_win, a_win, u_t, picked_d, w1_q, v_w, v_s = {}, {}, {}, {}, {}, {}, {}, {}
+
+        def products_db(c):
+            m = slice(P * c, P * (c + 1))
+            d_win[c] = product(
+                c, [(w3_wd[:, m].bitcast(FP8X4), w3_sd[:].bitcast(U8)[:, m], v3_w, v3_s)], "d_win")
+            b_win[c] = product(
+                c, [(w2_wd[:].bitcast(U8)[:, 2 * P * c : 2 * P * (c + 1)].bitcast(FP4X4), w2_sd[:].bitcast(U8)[:, m],
+                     v2_w, v2_s)], "b_win")
+
+        def product_a(c):
+            b, m = c // 4, slice(P * (c % 4), P * (c % 4 + 1))
+            a_win[c] = product(
+                c, [(w1_q[a, b][0][:, m].bitcast(FP8X4), w1_q[a, b][1][:, m], v_w[a], v_s[0][4 * a :, :])
+                    for a in range(2)], "a_win")
+
+        def pick_d(c):
+            t = ring.tile([P, J], F32, name="picked_d", bufs=3)
+            nc.vector.tensor_copy(t[:], d_win[c][:].indirect(pos3_t[:]))
+            picked_d[c] = t
+
+        def tanh_d(c):
+            u_t[c] = held([P, J], F32, "u%d" % c)
+            nc.scalar.activation(u_t[c][:], picked_d[c][:], ACT.Tanh)
+
+        def join_db(c):
+            t = ring.tile([P, J], F32, name="rel_b", bufs=2)
+            nc.vector.tensor_tensor(t[:], b_win[c][:].indirect(pos2_t[:]), rel_t[c][:], ALU.mult)
+            nc.vector.scalar_tensor_tensor(
+                u_t[c][:], u_t[c][:], gain_t[:, c : c + 1], t[:], ALU.mult, ALU.subtract)
+
+        cast_w1(0, 0)
+        casts = {2: (1, 0), 4: (0, 1), 6: (1, 1)}
+        for s in range(TILES + 2):
+            if s < TILES:
+                products_db(s)
+            if s in casts:
+                cast_w1(*casts[s])
+            if 1 <= s <= TILES:
+                pick_d(s - 1)
+            if s == 7:
+                v_s[0] = gather(tab_s, offs_t, U8, "v_s")
+                for a in range(2):
+                    v_w[a] = gather(tab_w[a], offs_t, U32, "v_w%d" % a)
+                for a in range(2):
+                    w1_q[a, 0] = quantize(w1_bf[a, 0][:], "w1q%d0" % a)
+            if s == 8:
+                for a in range(2):
+                    w1_q[a, 1] = quantize(w1_bf[a, 1][:], "w1q%d1" % a)
+            if s >= 8:
+                product_a(s - 8)
+            if s >= 2:
+                tanh_d(s - 2)
+                join_db(s - 2)
+
+        w4_bf = ring.tile([P, 2, N, 4], BF16, name="bf", bufs=3, align_bytes=64)
+        nc.scalar.copy(
+            w4_bf[:].rearrange("p b (c i) t -> p b c t i", i=4),
+            w4_raw[:].rearrange("p b t (c i) -> p b c t i", i=4),
+        )
+        w4_w, w4_s = quantize(w4_bf[:].rearrange("p b n t -> p (b n t)"), "w4q")
+
+        def weave(copy, z, width, name):
+            t = ring.tile([P, width, 4], BF16, name="bf", bufs=3, align_bytes=64)
+            copy(t[:].rearrange("p (c i) t -> p c t i", i=4), z[:].rearrange("p t (c i) -> p c t i", i=4))
+            return quantize(t[:].rearrange("p j t -> p (j t)"), name)
+
+        z0 = ring.tile([P, 4, J], F32, name="raw")
+        for t in range(4):
+            product_a(t + 2)
+            nc.vector.tensor_tensor(z0[:, t, :], a_win[t][:].indirect(pos1_t[:]), u_t[t][:], ALU.subtract)
+        product_a(6)
+        product_a(7)
+        z0_w, z0_s = weave(nc.scalar.copy, z0, J, "z0q")
+        out_v = out.rearrange("(m p) j -> p m j", p=P)
+        for h in range(2):
+            cols = slice(HALF * h, HALF * (h + 1))
+            z1 = ring.tile([P, 4, HALF], F32, name="raw")
+            for t in range(4):
+                nc.vector.tensor_tensor(
+                    z1[:, t, :], a_win[4 + t][:].indirect(pos1_t[:, HALF // 16 * h : HALF // 16 * (h + 1)]),
+                    u_t[4 + t][:, cols], ALU.subtract)
+            z1_w, z1_s = weave(nc.vector.tensor_copy if h else nc.scalar.copy, z1, HALF, "z1q%d" % h)
+            res = held([P, 2, HALF], F32, "res%d" % h)
+            for m in range(2):
+                acc = psum.tile([P, HALF], F32, name="bank")
+                for b, (zw, zs) in enumerate(((z0_w[:, cols], z0_s[:, cols]), (z1_w[:], z1_s[:]))):
+                    n_cols = slice(N * b + P * m, N * b + P * (m + 1))
+                    nc.tensor.matmul_mx(
+                        out=acc[:], lhsT=w4_w[:, n_cols].bitcast(FP8X4), lhsT_scale=w4_s[:, n_cols],
+                        rhs=zw.bitcast(FP8X4), rhs_scale=zs, start=(b == 0), stop=(b == 1),
+                    )
+                nc.scalar.activation(res[:, m, :], acc[:], ACT.Abs)
+            nc.sync.dma_start(out_v[:, :, cols], res[:])

@@ -69,21 +69,6 @@ def tile_list_deposit_suspicion_scores_kernel(
             )
             return t
 
-        offs3_t = load_list(offs3, "offs3_t")
-        tab3_s = held([P, T], U8, "tab3_s")
-        rows3 = tab3_scales.bitcast(I32)
-        for q in range(4):
-            nc.scalar.dma_start(
-                tab3_s[32 * q : 32 * q + 32, :].bitcast(I32),
-                rows3[:, 4 * q : 4 * q + 4, :].to_broadcast([8, 4, T // 4]),
-            )
-        tab3_w = load_words(tab3_words[0], "tab3_w")
-        w3_w = load_words(w3_words[0], "w3_w")
-        offs2_t = load_list(offs2, "offs2_t")
-        w3_s = load_scales(nc.scalar, nc.vector, w3_scales, "w3_s")
-        tab2_s = load_scales(nc.scalar, nc.vector, tab2_scales, "tab2_s")
-        w2_s = load_scales(nc.scalar, nc.vector, w2_scales, "w2_s")
-
         w1_raw = {}
 
         def load_w1(a, b):
@@ -93,11 +78,33 @@ def tile_list_deposit_suspicion_scores_kernel(
             )
             w1_raw[a, b] = t
 
-        tab2_w = load_words(tab2_words[0], "tab2_w")
+        rel_v = rel.rearrange("(b q t i) j -> b t q i j", b=2, q=16, t=4)
+        rel_t = []
+
+        def load_rel(c):
+            t = held([P, J], F32, "rel%d" % c)
+            nc.sync.dma_start(t[:], rel_v[c // 4, c % 4])
+            rel_t.append(t)
+
+        offs3_t = load_list(offs3, "offs3_t")
+        tab3_s = held([P, T], U8, "tab3_s")
+        rows3 = tab3_scales.bitcast(I32)
+        for q in range(4):
+            nc.sync.dma_start(
+                tab3_s[32 * q : 32 * q + 32, :].bitcast(I32),
+                rows3[:, 4 * q : 4 * q + 4, :].to_broadcast([8, 4, T // 4]),
+            )
+        tab3_w = load_words(tab3_words[0], "tab3_w")
+        w3_w = load_words(w3_words[0], "w3_w")
+        offs2_t = load_list(offs2, "offs2_t")
+        w3_s = load_scales(nc.sync, nc.vector, w3_scales, "w3_s")
         load_w1(0, 0)
+        tab2_s = load_scales(nc.sync, nc.vector, tab2_scales, "tab2_s")
+        tab2_w = load_words(tab2_words[0], "tab2_w")
         w2_w = held([P, 2 * H], U8, "w2_w")
         nc.sync.dma_start(w2_w[:].bitcast(I32), w2_words[0].bitcast(I32))
         pos3_t = load_list(pos3, "pos3_t")
+        w2_s = load_scales(nc.sync, nc.vector, w2_scales, "w2_s")
         pos2_t = load_list(pos2, "pos2_t")
 
         gain_rows = held([P, P], F32, "gain_rows")
@@ -108,29 +115,21 @@ def tile_list_deposit_suspicion_scores_kernel(
         ident = held([P, P], F32, "ident")
         make_identity(nc, ident[:])
 
-        rel_v = rel.rearrange("(b q t i) j -> b t q i j", b=2, q=16, t=4)
-        rel_t = []
-
-        def load_rel(c):
-            t = held([P, J], F32, "rel%d" % c)
-            nc.sync.dma_start(t[:], rel_v[c // 4, c % 4])
-            rel_t.append(t)
-
         load_rel(0)
         load_rel(1)
         load_w1(1, 0)
+        offs_t = load_list(offs, "offs_t")
+        tab_s = load_scales(nc.sync, nc.gpsimd, tab_scales, "tab_s")
+        tab_w = [load_words(tab_words[a], "tab_w%d" % a) for a in range(2)]
         load_rel(2)
         load_rel(3)
-        offs_t = load_list(offs, "offs_t")
-        pos1_t = load_list(pos1, "pos1_t")
         load_w1(0, 1)
         load_rel(4)
         load_rel(5)
         load_w1(1, 1)
+        pos1_t = load_list(pos1, "pos1_t")
         load_rel(6)
         load_rel(7)
-        tab_s = load_scales(nc.sync, nc.gpsimd, tab_scales, "tab_s")
-        tab_w = [load_words(tab_words[a], "tab_w%d" % a) for a in range(2)]
         w4_raw = ring.tile([P, 2, 4, N], F32, name="raw")
         w4_v = w4.rearrange("(b q t i) n -> b t q i n", b=2, q=16, t=4)
         for c in range(TILES):
@@ -154,7 +153,7 @@ def tile_list_deposit_suspicion_scores_kernel(
         w2_sd = deal(w2_s, "w2_sd")
 
         def product(c, passes, name):
-            win = ring.tile([P, S], F32, name=name)
+            win = ring.tile([P, S], F32, name="win", bufs=12)
             for h in range(S // BANK):
                 cols = slice(BANK * h, BANK * (h + 1))
                 acc = psum.tile([P, BANK], F32, name="bank")
@@ -185,10 +184,13 @@ def tile_list_deposit_suspicion_scores_kernel(
 
         d_win, b_win, a_win, u_t, picked_d, w1_q, v_w, v_s = {}, {}, {}, {}, {}, {}, {}, {}
 
-        def products_db(c):
+        def product_d(c):
             m = slice(P * c, P * (c + 1))
             d_win[c] = product(
                 c, [(w3_wd[:, m].bitcast(FP8X4), w3_sd[:].bitcast(U8)[:, m], v3_w, v3_s)], "d_win")
+
+        def product_b(c):
+            m = slice(P * c, P * (c + 1))
             b_win[c] = product(
                 c, [(w2_wd[:].bitcast(U8)[:, 2 * P * c : 2 * P * (c + 1)].bitcast(FP4X4), w2_sd[:].bitcast(U8)[:, m],
                      v2_w, v2_s)], "b_win")
@@ -200,7 +202,7 @@ def tile_list_deposit_suspicion_scores_kernel(
                     for a in range(2)], "a_win")
 
         def pick_d(c):
-            t = ring.tile([P, J], F32, name="picked_d", bufs=3)
+            t = ring.tile([P, J], F32, name="picked_d", bufs=4)
             nc.vector.tensor_copy(t[:], d_win[c][:].indirect(pos3_t[:]))
             picked_d[c] = t
 
@@ -209,66 +211,65 @@ def tile_list_deposit_suspicion_scores_kernel(
             nc.scalar.activation(u_t[c][:], picked_d[c][:], ACT.Tanh)
 
         def join_db(c):
-            t = ring.tile([P, J], F32, name="rel_b", bufs=2)
+            t = ring.tile([P, J], F32, name="rel_b", bufs=4)
             nc.vector.tensor_tensor(t[:], b_win[c][:].indirect(pos2_t[:]), rel_t[c][:], ALU.mult)
             nc.vector.scalar_tensor_tensor(
                 u_t[c][:], u_t[c][:], gain_t[:, c : c + 1], t[:], ALU.mult, ALU.subtract)
 
+        LEAD = 3
         cast_w1(0, 0)
-        casts = {2: (1, 0), 4: (0, 1), 6: (1, 1)}
-        for s in range(TILES + 2):
-            if s < TILES:
-                products_db(s)
-            if s in casts:
-                cast_w1(*casts[s])
-            if 1 <= s <= TILES:
-                pick_d(s - 1)
-            if s == 7:
+        w1_q[0, 0] = quantize(w1_bf[0, 0][:], "w1q00")
+        for c in range(LEAD):
+            product_d(c)
+        for c in range(LEAD):
+            pick_d(c)
+        casts = {1: [(1, 0)], 3: [(0, 1)], 5: [(1, 1)]}
+        for s in range(TILES):
+            product_b(s)
+            tanh_d(s)
+            if s == 2:
                 v_s[0] = gather(tab_s, offs_t, U8, "v_s")
                 for a in range(2):
                     v_w[a] = gather(tab_w[a], offs_t, U32, "v_w%d" % a)
-                for a in range(2):
-                    w1_q[a, 0] = quantize(w1_bf[a, 0][:], "w1q%d0" % a)
-            if s == 8:
-                for a in range(2):
-                    w1_q[a, 1] = quantize(w1_bf[a, 1][:], "w1q%d1" % a)
-            if s >= 8:
-                product_a(s - 8)
-            if s >= 2:
-                tanh_d(s - 2)
-                join_db(s - 2)
-
-        w4_bf = ring.tile([P, 2, N, 4], BF16, name="bf", bufs=3, align_bytes=64)
-        nc.scalar.copy(
-            w4_bf[:].rearrange("p b (c i) t -> p b c t i", i=4),
-            w4_raw[:].rearrange("p b t (c i) -> p b c t i", i=4),
-        )
-        w4_w, w4_s = quantize(w4_bf[:].rearrange("p b n t -> p (b n t)"), "w4q")
+            for ab in casts.get(s, []):
+                cast_w1(*ab)
+                w1_q[ab] = quantize(w1_bf[ab][:], "w1q%d%d" % ab)
+            if s + LEAD < TILES:
+                product_d(s + LEAD)
+            join_db(s)
+            if s + LEAD < TILES:
+                pick_d(s + LEAD)
 
         def weave(copy, z, width, name):
             t = ring.tile([P, width, 4], BF16, name="bf", bufs=3, align_bytes=64)
             copy(t[:].rearrange("p (c i) t -> p c t i", i=4), z[:].rearrange("p t (c i) -> p c t i", i=4))
             return quantize(t[:].rearrange("p j t -> p (j t)"), name)
 
+        for c in range(TILES):
+            product_a(c)
+        w4_bf = ring.tile([P, 2, N, 4], BF16, name="bf", bufs=3, align_bytes=64)
+        nc.scalar.copy(
+            w4_bf[:].rearrange("p b (c i) t -> p b c t i", i=4),
+            w4_raw[:].rearrange("p b t (c i) -> p b c t i", i=4),
+        )
         z0 = ring.tile([P, 4, J], F32, name="raw")
         for t in range(4):
-            product_a(t + 2)
             nc.vector.tensor_tensor(z0[:, t, :], a_win[t][:].indirect(pos1_t[:]), u_t[t][:], ALU.subtract)
-        product_a(6)
-        product_a(7)
+        w4_w, w4_s = quantize(w4_bf[:].rearrange("p b n t -> p (b n t)"), "w4q")
         z0_w, z0_s = weave(nc.scalar.copy, z0, J, "z0q")
         out_v = out.rearrange("(m p) j -> p m j", p=P)
-        for h in range(2):
-            cols = slice(HALF * h, HALF * (h + 1))
-            z1 = ring.tile([P, 4, HALF], F32, name="raw")
+        pieces = [(0, 256), (256, 384), (384, 512)]
+        for j0, j1 in pieces:
+            cols, width = slice(j0, j1), j1 - j0
+            z1 = ring.tile([P, 4, width], F32, name="raw")
             for t in range(4):
                 nc.vector.tensor_tensor(
-                    z1[:, t, :], a_win[4 + t][:].indirect(pos1_t[:, HALF // 16 * h : HALF // 16 * (h + 1)]),
+                    z1[:, t, :], a_win[4 + t][:].indirect(pos1_t[:, j0 // 16 : j1 // 16]),
                     u_t[4 + t][:, cols], ALU.subtract)
-            z1_w, z1_s = weave(nc.vector.tensor_copy if h else nc.scalar.copy, z1, HALF, "z1q%d" % h)
-            res = held([P, 2, HALF], F32, "res%d" % h)
+            z1_w, z1_s = weave(nc.vector.tensor_copy if j1 == J else nc.scalar.copy, z1, width, "z1q%d" % j0)
+            res = held([P, 2, width], F32, "res%d" % j0)
             for m in range(2):
-                acc = psum.tile([P, HALF], F32, name="bank")
+                acc = psum.tile([P, width], F32, name="bank")
                 for b, (zw, zs) in enumerate(((z0_w[:, cols], z0_s[:, cols]), (z1_w[:], z1_s[:]))):
                     n_cols = slice(N * b + P * m, N * b + P * (m + 1))
                     nc.tensor.matmul_mx(

from contextlib import ExitStack

import concourse.mybir as mybir
from concourse.masks import make_identity

T, S, J, K1, K2, K3, H, N = 2048, 1024, 512, 1024, 512, 512, 1024, 256
FLOPS = 2 * H * S * (K1 + K2 + K3) + 2 * H * N * J

F32 = mybir.dt.float32
BF16 = mybir.dt.bfloat16
I32 = mybir.dt.int32
U32 = mybir.dt.uint32
U16 = mybir.dt.uint16
U8 = mybir.dt.uint8
FP8X4 = mybir.dt.float8_e4m3fn_x4
FP4X4 = mybir.dt.float4_e2m1fn_x4
ACT = mybir.ActivationFunctionType
ALU = mybir.AluOpType

P = 128
BANK = 512
TILES = H // P
HALF = J // 2


def tile_list_deposit_suspicion_scores_kernel(
    tc, tab_words, tab_scales, tab2_words, tab2_scales, tab3_words, tab3_scales, offs, offs2, offs3,
    pos1, pos2, pos3, w1, w2_words, w2_scales, w3_words, w3_scales, rel, gain, w4, out,
):
    nc = tc.nc
    with ExitStack() as ctx:
        keep = ctx.enter_context(tc.tile_pool(name="keep", bufs=1))
        ring = ctx.enter_context(tc.tile_pool(name="ring", bufs=4))
        psum = ctx.enter_context(tc.psum_pool(name="psum", bufs=8))

        def held(shape, dtype, name):
            return keep.tile(shape, dtype, name=name, align_bytes=64)

        def load_list(src, name):
            t = keep.tile([P, src.shape[1]], U16, name=name)
            nc.sync.dma_start(t[:], src)
            return t

        def load_words(src, name):
            t = held([P, src.shape[1]], U32, name)
            nc.sync.dma_start(t[:].bitcast(I32), src.rearrange("p n i -> p (n i)").bitcast(I32))
            return t

        def load_scales(queue, zeroer, src, name):
            passes, width = src.shape[0], src.shape[2]
            t = held([P, width], U8, name)
            zeroer.memset(t[:].bitcast(I32), 0)
            rows = src.bitcast(I32)
            for q in range(4):
                queue.dma_start(t[32 * q : 32 * q + 4 * passes, :].bitcast(I32), rows[:, 4 * q : 4 * q + 4, :])
            return t

        def gather(window, lst, dtype, name):
            t = held([P, S], dtype, name)
            nc.vector.tensor_copy(t[:], window[:].indirect(lst[:]))
            return t

        def deal(src, name):
            words = src[:].bitcast(I32)
            t = held([P, words.shape[1]], I32, name)
            nc.vector.tensor_copy(
                t[:].rearrange("p (b t q i) -> p b t q i", b=2, t=4, q=16),
                words.rearrange("p (b q t i) -> p b t q i", b=2, t=4, q=16),
            )
            return t

        w1_raw = {}

        def load_w1(a, b):
            t = ring.tile([P, 4, BANK], F32, name="raw")
            nc.sync.dma_start(
                t[:], w1[512 * a : 512 * (a + 1), BANK * b : BANK * (b + 1)].rearrange("(p e) c -> p e c", e=4)
            )
            w1_raw[a, b] = t

        rel_v = rel.rearrange("(b q t i) j -> b t q i j", b=2, q=16, t=4)
        rel_t = []

        def load_rel(c):
            t = held([P, J], F32, "rel%d" % c)
            nc.sync.dma_start(t[:], rel_v[c // 4, c % 4])
            rel_t.append(t)

        offs3_t = load_list(offs3, "offs3_t")
        tab3_s = held([P, T], U8, "tab3_s")
        rows3 = tab3_scales.bitcast(I32)
        for q in range(4):
            nc.sync.dma_start(
                tab3_s[32 * q : 32 * q + 32, :].bitcast(I32),
                rows3[:, 4 * q : 4 * q + 4, :].to_broadcast([8, 4, T // 4]),
            )
        tab3_w = load_words(tab3_words[0], "tab3_w")
        w3_w = load_words(w3_words[0], "w3_w")
        offs2_t = load_list(offs2, "offs2_t")
        w3_s = load_scales(nc.sync, nc.vector, w3_scales, "w3_s")
        load_w1(0, 0)
        tab2_s = load_scales(nc.sync, nc.vector, tab2_scales, "tab2_s")
        tab2_w = load_words(tab2_words[0], "tab2_w")
        w2_w = held([P, 2 * H], U8, "w2_w")
        nc.sync.dma_start(w2_w[:].bitcast(I32), w2_words[0].bitcast(I32))
        pos3_t = load_list(pos3, "pos3_t")
        w2_s = load_scales(nc.sync, nc.vector, w2_scales, "w2_s")
        pos2_t = load_list(pos2, "pos2_t")

        gain_rows = held([P, P], F32, "gain_rows")
        nc.gpsimd.memset(gain_rows[:], 0.0)
        gain_v = gain.rearrange("(b q t i) -> b t q i", b=2, q=16, t=4)
        for b in range(2):
            nc.gpsimd.dma_start(gain_rows[4 * b : 4 * b + 4, :].rearrange("t (q i) -> t q i", q=16), gain_v[b])
        ident = held([P, P], F32, "ident")
        make_identity(nc, ident[:])

        load_rel(0)
        load_rel(1)
        load_w1(1, 0)
        offs_t = load_list(offs, "offs_t")
        tab_s = load_scales(nc.sync, nc.gpsimd, tab_scales, "tab_s")
        tab_w = [load_words(tab_words[a], "tab_w%d" % a) for a in range(2)]
        load_rel(2)
        load_rel(3)
        load_w1(0, 1)
        load_rel(4)
        load_rel(5)
        load_w1(1, 1)
        pos1_t = load_list(pos1, "pos1_t")
        load_rel(6)
        load_rel(7)
        w4_raw = ring.tile([P, 2, 4, N], F32, name="raw")
        w4_v = w4.rearrange("(b q t i) n -> b t q i n", b=2, q=16, t=4)
        for c in range(TILES):
            nc.sync.dma_start(w4_raw[:, c // 4, c % 4, :], w4_v[c // 4, c % 4])

        warm = held([P, 8], F32, "warm")
        nc.scalar.activation(warm[:, 0:1], ident[:, 0:1], ACT.Tanh)

        gain_ps = psum.tile([P, BANK], F32, name="bank")
        nc.tensor.transpose(gain_ps[:, 0:P], gain_rows[:], ident[:])
        gain_t = held([P, TILES], F32, "gain_t")
        nc.scalar.copy(gain_t[:], gain_ps[:, 0:TILES])

        v3_s = gather(tab3_s, offs3_t, U8, "v3_s")
        v3_w = gather(tab3_w, offs3_t, U32, "v3_w")
        w3_wd = deal(w3_w, "w3_wd")
        w3_sd = deal(w3_s, "w3_sd")
        v2_s = gather(tab2_s, offs2_t, U8, "v2_s")
        v2_w = gather(tab2_w, offs2_t, U32, "v2_w")
        w2_wd = deal(w2_w, "w2_wd")
        w2_sd = deal(w2_s, "w2_sd")

        def product(c, passes, name):
            win = ring.tile([P, S], F32, name="win", bufs=12)
            for h in range(S // BANK):
                cols = slice(BANK * h, BANK * (h + 1))
                acc = psum.tile([P, BANK], F32, name="bank")
                for n, (lw, ls, rw, rs) in enumerate(passes):
                    nc.tensor.matmul_mx(
                        out=acc[:], lhsT=lw, lhsT_scale=ls, rhs=rw[:, cols].bitcast(FP8X4), rhs_scale=rs[:, cols],
                        start=(n == 0), stop=(n == len(passes) - 1),
                    )
                nc.scalar.copy(win[:, cols], acc[:])
            return win

        w1_bf = {}

        def cast_w1(a, b):
            t = ring.tile([P, 4 * BANK], BF16, name="bf", bufs=3, align_bytes=64)
            nc.scalar.copy(
                t[:].rearrange("p (t q i e) -> p t q e i", t=4, q=16, e=4),
                w1_raw[a, b][:].rearrange("p e (q t i) -> p t q e i", t=4, q=16),
            )
            w1_bf[a, b] = t

        def quantize(src, name):
            width = src.shape[1] // 4
            codes = held([P, width], U32, name + "_w")
            scales = held([P, width], U8, name + "_s")
            nc.vector.quantize_mx(out=codes[:].bitcast(FP8X4), scales=scales[:], in_=src)
            return codes, scales

        d_win, b_win, a_win, u_t, picked_d, w1_q, v_w, v_s = {}, {}, {}, {}, {}, {}, {}, {}

        def product_d(c):
            m = slice(P * c, P * (c + 1))
            d_win[c] = product(
                c, [(w3_wd[:, m].bitcast(FP8X4), w3_sd[:].bitcast(U8)[:, m], v3_w, v3_s)], "d_win")

        def product_b(c):
            m = slice(P * c, P * (c + 1))
            b_win[c] = product(
                c, [(w2_wd[:].bitcast(U8)[:, 2 * P * c : 2 * P * (c + 1)].bitcast(FP4X4), w2_sd[:].bitcast(U8)[:, m],
                     v2_w, v2_s)], "b_win")

        def product_a(c):
            b, m = c // 4, slice(P * (c % 4), P * (c % 4 + 1))
            a_win[c] = product(
                c, [(w1_q[a, b][0][:, m].bitcast(FP8X4), w1_q[a, b][1][:, m], v_w[a], v_s[0][4 * a :, :])
                    for a in range(2)], "a_win")

        def pick_d(c):
            t = ring.tile([P, J], F32, name="picked_d", bufs=4)
            nc.vector.tensor_copy(t[:], d_win[c][:].indirect(pos3_t[:]))
            picked_d[c] = t

        def tanh_d(c):
            u_t[c] = held([P, J], F32, "u%d" % c)
            nc.scalar.activation(u_t[c][:], picked_d[c][:], ACT.Tanh)

        def join_db(c):
            t = ring.tile([P, J], F32, name="rel_b", bufs=4)
            nc.vector.tensor_tensor(t[:], b_win[c][:].indirect(pos2_t[:]), rel_t[c][:], ALU.mult)
            nc.vector.scalar_tensor_tensor(
                u_t[c][:], u_t[c][:], gain_t[:, c : c + 1], t[:], ALU.mult, ALU.subtract)

        LEAD = 3
        cast_w1(0, 0)
        w1_q[0, 0] = quantize(w1_bf[0, 0][:], "w1q00")
        for c in range(LEAD):
            product_d(c)
        for c in range(LEAD):
            pick_d(c)
        casts = {1: [(1, 0)], 3: [(0, 1)], 5: [(1, 1)]}
        for s in range(TILES):
            product_b(s)
            tanh_d(s)
            if s == 2:
                v_s[0] = gather(tab_s, offs_t, U8, "v_s")
                for a in range(2):
                    v_w[a] = gather(tab_w[a], offs_t, U32, "v_w%d" % a)
            for ab in casts.get(s, []):
                cast_w1(*ab)
                w1_q[ab] = quantize(w1_bf[ab][:], "w1q%d%d" % ab)
            if s + LEAD < TILES:
                product_d(s + LEAD)
            join_db(s)
            if s + LEAD < TILES:
                pick_d(s + LEAD)

        def weave(copy, z, width, name):
            t = ring.tile([P, width, 4], BF16, name="bf", bufs=3, align_bytes=64)
            copy(t[:].rearrange("p (c i) t -> p c t i", i=4), z[:].rearrange("p t (c i) -> p c t i", i=4))
            return quantize(t[:].rearrange("p j t -> p (j t)"), name)

        for c in range(TILES):
            product_a(c)
        w4_bf = ring.tile([P, 2, N, 4], BF16, name="bf", bufs=3, align_bytes=64)
        nc.scalar.copy(
            w4_bf[:].rearrange("p b (c i) t -> p b c t i", i=4),
            w4_raw[:].rearrange("p b t (c i) -> p b c t i", i=4),
        )
        z0 = ring.tile([P, 4, J], F32, name="raw")
        for t in range(4):
            nc.vector.tensor_tensor(z0[:, t, :], a_win[t][:].indirect(pos1_t[:]), u_t[t][:], ALU.subtract)
        w4_w, w4_s = quantize(w4_bf[:].rearrange("p b n t -> p (b n t)"), "w4q")
        z0_w, z0_s = weave(nc.scalar.copy, z0, J, "z0q")
        out_v = out.rearrange("(m p) j -> p m j", p=P)
        pieces = [(0, 256), (256, 384), (384, 512)]
        for j0, j1 in pieces:
            cols, width = slice(j0, j1), j1 - j0
            z1 = ring.tile([P, 4, width], F32, name="raw")
            for t in range(4):
                nc.vector.tensor_tensor(
                    z1[:, t, :], a_win[4 + t][:].indirect(pos1_t[:, j0 // 16 : j1 // 16]),
                    u_t[4 + t][:, cols], ALU.subtract)
            z1_w, z1_s = weave(nc.vector.tensor_copy if j1 == J else nc.scalar.copy, z1, width, "z1q%d" % j0)
            res = held([P, 2, width], F32, "res%d" % j0)
            for m in range(2):
                acc = psum.tile([P, width], F32, name="bank")
                for b, (zw, zs) in enumerate(((z0_w[:, cols], z0_s[:, cols]), (z1_w[:], z1_s[:]))):
                    n_cols = slice(N * b + P * m, N * b + P * (m + 1))
                    nc.tensor.matmul_mx(
                        out=acc[:], lhsT=w4_w[:, n_cols].bitcast(FP8X4), lhsT_scale=w4_s[:, n_cols],
                        rhs=zw.bitcast(FP8X4), rhs_scale=zs, start=(b == 0), stop=(b == 1),
                    )
                nc.scalar.activation(res[:, m, :], acc[:], ACT.Abs)
            nc.sync.dma_start(out_v[:, :, cols], res[:])
